import numpy as np
import ml_dtypes


def mxq(x, axis, fmt="e4m3"):
    dtype, down = {"e4m3": (ml_dtypes.float8_e4m3fn, 7), "e5m2": (ml_dtypes.float8_e5m2, 14)}[fmt]
    v = np.moveaxis(np.asarray(x, np.float32).astype(ml_dtypes.bfloat16).astype(np.float64), axis, -1)
    blocks = v.reshape(v.shape[:-1] + (-1, 32))
    amax = np.abs(blocks).max(-1, keepdims=True)
    byte = np.maximum(np.where(amax > 0, np.frexp(amax)[1] - 1 + 127, 0) - down, 1)
    scale = np.exp2(byte - 127.0)
    codes = (blocks / scale).astype(np.float32).astype(dtype).astype(np.float64)
    return np.moveaxis((codes * scale).reshape(v.shape), -1, axis)


WIDE = False


def mx_kscale(k):
    if not WIDE:
        return np.ones(k)
    levels = np.array([10, -10, 5, -5, 0])
    if k % 512:
        return np.exp2(np.random.permutation(np.resize(levels, k // 32))).repeat(32)
    a = np.empty((k // 512, 16))
    for p in range(k // 512):
        a[p, :8] = np.random.permutation(np.resize(levels, 8))
        for g in range(8):
            far = levels[np.abs(levels - a[p, g]) >= 10]
            a[p, g + 8] = far[np.random.randint(len(far))]
    return np.exp2(a.ravel()).repeat(32)


def f64(x):
    return np.asarray(x).astype(np.float64)


def striped(idx):
    return np.tile(idx.reshape(-1, 16).T, (8, 1)).astype(np.uint16)


def unstriped(offs):
    return offs[:16].T.reshape(-1).astype(np.int64)


E2M1 = np.array([0.0, 0.5, 1.0, 1.5, 2.0, 3.0, 4.0, 6.0, -0.0, -0.5, -1.0, -1.5, -2.0, -3.0, -4.0, -6.0])


def pack_weight(w, fmt):
    k, n = w.shape
    w = f64(np.asarray(w, np.float32).astype(ml_dtypes.bfloat16)).reshape(k // 32, 32, n)
    amax = np.abs(w).max(1)
    if fmt == "e4m3":
        byte = np.frexp(amax)[1] - 1 + 127 - 7
    else:
        mant, ex = np.frexp(amax / 6.0)
        byte = np.where(mant > 0.5, ex, ex - 1) + 127
    byte = np.clip(np.where(amax > 0, byte, 1), 1, 254)
    scaled = (w * np.exp2(127.0 - byte)[:, None, :]).reshape(k, n).astype(np.float32)
    by_word = np.ascontiguousarray(scaled.reshape(k // 512, 128, 4, n).transpose(0, 1, 3, 2))
    if fmt == "e4m3":
        words = by_word.astype(ml_dtypes.float8_e4m3fn).view(np.uint8)
    else:
        c = by_word.astype(ml_dtypes.float4_e2m1fn).view(np.uint8) & 0xF
        words = (c[..., 0::2] | (c[..., 1::2] << 4)).reshape(k // 512, 128, 2 * n)
    return np.ascontiguousarray(words), np.ascontiguousarray(byte.astype(np.uint8).reshape(k // 512, 16, n))


def unpack_weight(words, scales, fmt):
    g, _, n = scales.shape
    words = np.ascontiguousarray(words).reshape(g, 128, n, -1)
    if fmt == "e4m3":
        vals = words.view(ml_dtypes.float8_e4m3fn).astype(np.float64)
    else:
        nib = np.empty((g, 128, n, 4), np.uint8)
        nib[..., 0::2] = words & 0xF
        nib[..., 1::2] = words >> 4
        vals = E2M1[nib]
    vals = vals * np.repeat(np.exp2(scales.astype(np.float64) - 127.0), 8, axis=1)[..., None]
    return vals.transpose(0, 1, 3, 2).reshape(g * 512, n)


def gelu(v):
    return 0.5 * v * (1.0 + np.tanh(np.sqrt(2.0 / np.pi) * (v + 0.044715 * v**3)))


def bf(x):
    return np.asarray(x, np.float32).astype(ml_dtypes.bfloat16)


def planes(Y):
    n, m = Y.shape
    b = f64(bf(Y)).reshape(n // 32, 32, m)
    amax = np.abs(b).max(1)
    byte = np.clip(np.where(amax > 0, np.frexp(amax)[1] - 1 + 127 - 7, 1), 1, 254)
    codes = (b * np.exp2(127.0 - byte)[:, None, :]).reshape(n, m).astype(np.float32).astype(ml_dtypes.float8_e4m3fn).view(np.uint8)
    words = codes.reshape(n // 512, 128, 4, m).transpose(0, 1, 3, 2)
    return np.ascontiguousarray(words), np.ascontiguousarray(byte.astype(np.uint8).reshape(n // 512, 16, m))


K, T, S, H, M, N, P = 512, 4096, 1024, 1024, 512, 512, 512

def setup_inputs():
    n = np.random.standard_normal
    s = mx_kscale(K)[:, None]
    u = mx_kscale(H)[:, None]
    u3 = mx_kscale(M)[:, None]
    size = np.sqrt(np.exp(0.8 * n(N)))[None, :]
    d = {}
    d["tab_words"], d["tab_scales"] = pack_weight(n((K, T)) * s, "e4m3")
    d["offs"] = striped(np.random.permutation(T)[:S])
    d["pos1"] = striped(np.random.permutation(S)[:P])
    d["pos2"] = striped(np.random.permutation(S)[:P])
    d["w1"] = (n((K, H)) / K**0.5 / s).astype(np.float32)
    d["w2"] = (n((K, H)) / K**0.5 / s).astype(np.float32)
    d["gain"] = (np.exp(0.3 * n(H)) * u[:, 0]).astype(np.float32)
    d["w3_words"], d["w3_scales"] = pack_weight(n((K, M)) / K**0.5 / s * u3.T, "e4m3")
    d["load"] = n((M, S)).astype(np.float32)
    d["w4_words"], d["w4_scales"] = pack_weight(0.8 * n((H, N)) / H**0.5 / u * size, "e2m1")
    d["w5"] = (n((M, N)) / M**0.5 / u3 * size).astype(np.float32)
    return d

def reference(tab_words, tab_scales, offs, pos1, pos2, w1, w2, gain, w3_words, w3_scales, load, w4_words, w4_scales, w5):
    v = unpack_weight(tab_words, tab_scales, "e4m3")[:, unstriped(offs)]
    re = mxq(f64(w1), 0, "e4m3").T @ v
    im = mxq(f64(w2), 0, "e4m3").T @ v
    h = np.sqrt(np.square(re) + np.square(im)) * f64(gain)[:, None]
    b = (unpack_weight(w3_words, w3_scales, "e4m3").T @ v) * f64(load)
    hq = mxq(h, 0, "e4m3")
    bq = mxq(b, 0, "e4m3")
    w4 = unpack_weight(w4_words, w4_scales, "e2m1")
    g2 = w4.T @ hq + mxq(f64(w5), 0, "e4m3").T @ bq
    y = g2[:, unstriped(pos1)] * g2[:, unstriped(pos2)]
    words, scales = planes(y)
    return y, words, scales

@@ -1,0 +1,288 @@
+from contextlib import ExitStack
+
+import concourse.mybir as mybir
+
+K, T, S, H, M, N, PAIRS = 512, 4096, 1024, 1024, 512, 512, 512
+FLOPS = 2 * K * S * (2 * H + M) + 2 * S * N * (H + M)
+
+F32 = mybir.dt.float32
+BF16 = mybir.dt.bfloat16
+I32 = mybir.dt.int32
+U32 = mybir.dt.uint32
+U16 = mybir.dt.uint16
+U8 = mybir.dt.uint8
+FP8X4 = mybir.dt.float8_e4m3fn_x4
+FP4X4 = mybir.dt.float4_e2m1fn_x4
+ALU = mybir.AluOpType
+ACT = mybir.ActivationFunctionType
+
+P = 128
+PACK = 4
+PASS = P * PACK
+HALF = 512
+LIST_ROWS = 16
+QUADS = 4
+SIGN_COLS = 64
+PAIR_PIECES = (256, 128, 128)
+
+
+def tile_list_electrolyser_sweep_pairs_kernel(
+    tc, tab_words, tab_scales, offs, pos1, pos2, w1, w2, gain, w3_words, w3_scales, load,
+    w4_words, w4_scales, w5, out_0, out_1, out_2,
+):
+    nc = tc.nc
+    with ExitStack() as ctx:
+        keep = ctx.enter_context(tc.tile_pool(name="keep", bufs=1))
+        stage = ctx.enter_context(tc.tile_pool(name="stage", bufs=1))
+        work = ctx.enter_context(tc.tile_pool(name="work", bufs=2))
+        psum = ctx.enter_context(tc.psum_pool(name="psum", bufs=4))
+
+        def kept(shape, dtype, name):
+            return keep.tile(shape, dtype, name=name, align_bytes=64)
+
+        def load_rows(src, slot):
+            raw = stage.tile([P, PACK, HALF], F32, name="raw", tag=slot)
+            nc.sync.dma_start(out=raw[:], in_=src.rearrange("(p j) c -> p j c", j=PACK))
+            return raw
+
+        def round_weight(raw, copy):
+            wb = work.tile([P, PACK * PASS], BF16, name="wb", align_bytes=64)
+            copy(
+                out=wb[:].rearrange("p (t m j) -> p m j t", t=PACK, j=PACK),
+                in_=raw[:].rearrange("p j (m t) -> p m j t", t=PACK),
+            )
+            return wb
+
+        def quantise(src, name):
+            width = src.shape[1] // PACK
+            codes = kept([P, width], U32, name + "_codes")
+            scales = kept([P, width], U8, name + "_scales")
+            nc.vector.quantize_mx(out=codes[:].bitcast(FP8X4), scales=scales[:], in_=src)
+            return codes, scales
+
+        def woven(ap):
+            return ap.rearrange("p (c i t) -> p c t i", t=PACK, i=PACK)
+
+        def planes(ap):
+            return ap.rearrange("p t (c i) -> p c t i", i=PACK)
+
+        def cols(t):
+            return slice(t * P, (t + 1) * P)
+
+        tab_s = stage.tile([P, T], U8, name="tab_s", tag="c")
+        nc.vector.memset(tab_s[:].bitcast(I32), 0)
+        ws_raw = kept([P, 2, PASS], U8, "ws_raw")
+        nc.gpsimd.memset(ws_raw[:].bitcast(I32), 0)
+
+        offs_t = keep.tile([P, S // LIST_ROWS], U16, name="offs_t")
+        nc.sync.dma_start(offs_t[:], offs)
+        gain_t = kept([P, 2, PACK], F32, "gain_t")
+        nc.sync.dma_start(out=gain_t[:], in_=gain.rearrange("(b p t) -> p b t", b=2, t=PACK))
+        pos_t = []
+        for name, src in (("pos1_t", pos1), ("pos2_t", pos2)):
+            pos_t.append(keep.tile([P, PAIRS // LIST_ROWS], U16, name=name))
+            nc.sync.dma_start(pos_t[-1][:], src)
+        raw_1a = load_rows(w1[:, 0:PASS], "a")
+        for q in range(QUADS):
+            nc.scalar.dma_start(
+                out=tab_s[32 * q : 32 * q + 4, :].bitcast(I32),
+                in_=tab_scales[0, 4 * q : 4 * q + 4, :].bitcast(I32),
+            )
+        tab_w = stage.tile([P, T], I32, name="tab_w", tag="d")
+        nc.sync.dma_start(out=tab_w[:], in_=tab_words[0].rearrange("p t i -> p (t i)").bitcast(I32))
+
+        for q in range(QUADS):
+            nc.gpsimd.dma_start(
+                out=ws_raw[32 * q : 32 * q + 4, :, :].bitcast(I32),
+                in_=w4_scales[:, 4 * q : 4 * q + 4, :].rearrange("a r c -> r a c").bitcast(I32),
+            )
+            nc.gpsimd.dma_start(
+                out=ws_raw[32 * q + 4 : 32 * q + 8, 0, :].bitcast(I32),
+                in_=w3_scales[0, 4 * q : 4 * q + 4, :].bitcast(I32),
+            )
+
+        twice = stage.tile([P, 2, PACK], F32, name="twice", tag="b")
+        nc.vector.tensor_scalar(twice[:], gain_t[:], 0.0, 2.0, ALU.is_ge, ALU.mult)
+        sign = kept([P, 2, SIGN_COLS, PACK], BF16, "sign")
+        nc.vector.tensor_scalar(
+            sign[:], twice[:].unsqueeze(2).to_broadcast([P, 2, SIGN_COLS, PACK]), -1.0, None, ALU.add
+        )
+
+        raw_2a = load_rows(w2[:, 0:PASS], "b")
+        w1q = {0: quantise(round_weight(raw_1a, nc.scalar.copy)[:], "w1a")}
+        v_s = [kept([P, HALF], U8, "v_s%d" % s) for s in range(2)]
+        v_w = [kept([P, HALF], U32, "v_w%d" % s) for s in range(2)]
+
+        def gather_words(s):
+            per = HALF // LIST_ROWS
+            entries = offs_t[:, s * per : (s + 1) * per]
+            nc.vector.tensor_copy(v_s[s][:], tab_s[:].indirect(entries))
+            nc.vector.tensor_copy(v_w[s][:], tab_w[:].bitcast(U32).indirect(entries))
+
+        gather_words(0)
+        w2q = {0: quantise(round_weight(raw_2a, nc.vector.tensor_copy)[:], "w2a")}
+        gather_words(1)
+
+        def stage1(out, wq, t, s, c0, width):
+            nc.tensor.matmul_mx(
+                out=out,
+                lhsT=wq[0][:, cols(t)].bitcast(FP8X4),
+                lhsT_scale=wq[1][:, cols(t)],
+                rhs=v_w[s][:, c0 : c0 + width].bitcast(FP8X4),
+                rhs_scale=v_s[s][:, c0 : c0 + width],
+                start=True,
+                stop=True,
+            )
+
+        def magnitudes(b, s, c0, width, order):
+            sq = [work.tile([P, PACK, width], F32, name="sq%d" % part) for part in range(2)]
+            for part, t in order:
+                bank = psum.tile([P, width], F32, name="reim")
+                stage1(bank[:], (w1q, w2q)[part][b], t, s, c0, width)
+                nc.scalar.activation(sq[part][:, t, :], bank[:], ACT.Square, scale=gain_t[:, b, t : t + 1])
+                if part == 1:
+                    nc.vector.tensor_tensor(sq[0][:, t, :], sq[0][:, t, :], sq[1][:, t, :], ALU.add)
+            hb = work.tile([P, PACK * width], BF16, name="hb", align_bytes=64)
+            nc.scalar.activation(woven(hb[:]), planes(sq[0][:]), ACT.Sqrt)
+            run = SIGN_COLS * PACK
+            reps = PACK * width // run
+            hv = hb[:].rearrange("p (r x) -> p r x", x=run)
+            nc.vector.tensor_tensor(
+                hv, hv,
+                sign[:, b].rearrange("p c t -> p (c t)").unsqueeze(1).to_broadcast([P, reps, run]),
+                ALU.mult,
+            )
+            return quantise(hb[:], "h%d%d_%d" % (b, s, c0))
+
+        re_first = [(part, t) for part in range(2) for t in range(PACK)]
+        in_turn = [(part, t) for t in range(PACK) for part in range(2)]
+
+        def weighted(s, load_raw, w3q):
+            bb = work.tile([P, PACK * HALF], BF16, name="bb", align_bytes=64)
+            for c in range(HALF // P):
+                bank = psum.tile([P, PACK, P], F32, name="acc")
+                for t in range(PACK):
+                    stage1(bank[:, t, :], w3q, t, s, c * P, P)
+                nc.vector.tensor_tensor(
+                    woven(bb[:, c * PASS : (c + 1) * PASS]),
+                    planes(bank[:]),
+                    planes(load_raw[:, :, cols(c)]),
+                    ALU.mult,
+                )
+            return quantise(bb[:], "b%d" % s)
+
+        hq = {}
+        hq[0, 0] = magnitudes(0, 0, 0, HALF, re_first)
+
+        raw_1b = load_rows(w1[:, PASS:H], "a")
+        raw_2b = load_rows(w2[:, PASS:H], "c")
+        w3_raw = stage.tile([P, M], I32, name="w3_raw", tag="b")
+        nc.sync.dma_start(out=w3_raw[:], in_=w3_words[0].rearrange("p c i -> p (c i)").bitcast(I32))
+        load_0 = load_rows(load[:, 0:HALF], "d")
+        w1q[1] = quantise(round_weight(raw_1b, nc.vector.tensor_copy)[:], "w1b")
+        w2q[1] = quantise(round_weight(raw_2b, nc.vector.tensor_copy)[:], "w2b")
+        raw_5 = load_rows(w5, "a")
+        load_1 = load_rows(load[:, HALF:S], "c")
+
+        ws = kept([P, 2, PASS], U8, "ws")
+        nc.vector.tensor_copy(
+            out=ws[:].rearrange("p a (t q) -> p a q t", t=PACK),
+            in_=ws_raw[:].rearrange("p a (q t) -> p a q t", t=PACK),
+        )
+        w3_w = kept([P, M], I32, "w3_w")
+        nc.vector.tensor_copy(
+            out=w3_w[:].rearrange("p (t q) -> p q t", t=PACK),
+            in_=w3_raw[:].rearrange("p (q t) -> p q t", t=PACK),
+        )
+        w3q = (w3_w, ws[4:P, 0, :])
+        w4_raw = stage.tile([P, 2, N // 2], I32, name="w4_raw", tag="b")
+        nc.sync.dma_start(out=w4_raw[:], in_=w4_words.rearrange("a p c -> p a c").bitcast(I32))
+
+        hq[0, 1] = magnitudes(0, 1, 0, HALF, in_turn)
+        bq = {0: weighted(0, load_0, w3q)}
+
+        hq[1, 0] = magnitudes(1, 0, 0, HALF, in_turn)
+        w5q = quantise(round_weight(raw_5, nc.vector.tensor_copy)[:], "w5")
+        w4_w = kept([P, 2, 2 * N], U8, "w4_w")
+        nc.vector.tensor_copy(
+            out=w4_w[:].bitcast(U16).rearrange("p a (t q) -> p a q t", t=PACK),
+            in_=w4_raw[:].bitcast(U16).rearrange("p a (q t) -> p a q t", t=PACK),
+        )
+        bq[1] = weighted(1, load_1, w3q)
+
+        g2 = [kept([P, S], F32, "g2_%d" % t) for t in range(PACK)]
+
+        def with_b(bank, t, s):
+            nc.tensor.matmul_mx(
+                out=bank[:],
+                lhsT=w5q[0][:, cols(t)].bitcast(FP8X4),
+                lhsT_scale=w5q[1][:, cols(t)],
+                rhs=bq[s][0][:].bitcast(FP8X4),
+                rhs_scale=bq[s][1][:],
+                start=True,
+                stop=False,
+            )
+
+        def with_h(out, t, b, h, last):
+            nc.tensor.matmul_mx(
+                out=out,
+                lhsT=w4_w[:, b, 2 * t * P : 2 * (t + 1) * P].bitcast(FP4X4),
+                lhsT_scale=ws[:, b, cols(t)],
+                rhs=h[0][:].bitcast(FP8X4),
+                rhs_scale=h[1][:],
+                start=False,
+                stop=last,
+            )
+
+        for t in range(PACK):
+            bank = psum.tile([P, HALF], F32, name="acc")
+            with_b(bank, t, 0)
+            with_h(bank[:], t, 0, hq[0, 0], False)
+            with_h(bank[:], t, 1, hq[1, 0], True)
+            nc.scalar.copy(g2[t][:, 0:HALF], bank[:])
+
+        quarter = HALF // 2
+        h_last = [magnitudes(1, 1, 0, quarter, in_turn)]
+        banks = []
+        for t in range(PACK):
+            banks.append(psum.tile([P, HALF], F32, name="acc"))
+            with_b(banks[t], t, 1)
+            with_h(banks[t][:], t, 0, hq[0, 1], False)
+            with_h(banks[t][:, 0:quarter], t, 1, h_last[0], False)
+        h_last.append(magnitudes(1, 1, quarter, quarter, in_turn))
+        for t in range(PACK):
+            with_h(banks[t][:, quarter:HALF], t, 1, h_last[1], True)
+            nc.scalar.copy(g2[t][:, HALF:S], banks[t][:])
+
+        y_codes = kept([P, PAIRS], U32, "y_codes")
+        y_scales = kept([P, PAIRS], U8, "y_scales")
+        out_rows = out_0.rearrange("(p t) j -> p t j", t=PACK)
+        out_words = out_1[0].rearrange("p m t -> p (m t)").bitcast(I32)
+        j0 = 0
+        for piece, width in enumerate(PAIR_PIECES):
+            entries = slice(j0 // LIST_ROWS, (j0 + width) // LIST_ROWS)
+            first = kept([P, PACK, width], F32, "first%d" % piece)
+            y = kept([P, PACK, width], F32, "y%d" % piece)
+            for t in range(PACK):
+                nc.vector.tensor_copy(first[:, t, :], g2[t][:].indirect(pos_t[0][:, entries]))
+            for t in range(PACK):
+                nc.vector.tensor_tensor(
+                    y[:, t, :], g2[t][:].indirect(pos_t[1][:, entries]), first[:, t, :], ALU.mult
+                )
+            nc.sync.dma_start(out=out_rows[:, :, j0 : j0 + width], in_=y[:])
+            yb = kept([P, PACK * width], BF16, "yb%d" % piece)
+            nc.scalar.copy(woven(yb[:]), planes(y[:]))
+            nc.vector.quantize_mx(
+                out=y_codes[:, j0 : j0 + width].bitcast(FP8X4),
+                scales=y_scales[:, j0 : j0 + width],
+                in_=yb[:],
+            )
+            nc.sync.dma_start(
+                out=out_words[:, j0 : j0 + width], in_=y_codes[:, j0 : j0 + width].bitcast(I32)
+            )
+            j0 = j0 + width
+        for q in range(QUADS):
+            (nc.sync, nc.scalar)[q % 2].dma_start(
+                out=out_2[0, 4 * q : 4 * q + 4, :].bitcast(I32),
+                in_=y_scales[32 * q : 32 * q + 4, :].bitcast(I32),
+            )

@@ -45,8 +45,9 @@ def tile_list_electrolyser_sweep_pairs_kernel(
             nc.sync.dma_start(out=raw[:], in_=src.rearrange("(p j) c -> p j c", j=PACK))
             return raw
 
-        def round_weight(raw, copy):
-            wb = work.tile([P, PACK * PASS], BF16, name="wb", align_bytes=64)
+        def round_weight(raw, copy, wb=None):
+            if wb is None:
+                wb = work.tile([P, PACK * PASS], BF16, name="wb", align_bytes=64)
             copy(
                 out=wb[:].rearrange("p (t m j) -> p m j t", t=PACK, j=PACK),
                 in_=raw[:].rearrange("p j (m t) -> p m j t", t=PACK),
@@ -120,7 +121,8 @@ def tile_list_electrolyser_sweep_pairs_kernel(
             nc.vector.tensor_copy(v_w[s][:], tab_w[:].bitcast(U32).indirect(entries))
 
         gather_words(0)
-        w2q = {0: quantise(round_weight(raw_2a, nc.vector.tensor_copy)[:], "w2a")}
+        wb_2a = stage.tile([P, PACK * PASS], BF16, name="wb_2a", tag="e", align_bytes=64)
+        w2q = {0: quantise(round_weight(raw_2a, nc.vector.tensor_copy, wb_2a)[:], "w2a")}
         gather_words(1)
 
         def stage1(out, wq, t, s, c0, width):
@@ -184,7 +186,7 @@ def tile_list_electrolyser_sweep_pairs_kernel(
         raw_5 = load_rows(w5, "a")
         load_1 = load_rows(load[:, HALF:S], "c")
 
-        ws = kept([P, 2, PASS], U8, "ws")
+        ws = stage.tile([P, 2, PASS], U8, name="ws", tag="e", align_bytes=64)
         nc.vector.tensor_copy(
             out=ws[:].rearrange("p a (t q) -> p a q t", t=PACK),
             in_=ws_raw[:].rearrange("p a (q t) -> p a q t", t=PACK),

@@ -34,6 +34,7 @@ def tile_list_electrolyser_sweep_pairs_kernel(
     with ExitStack() as ctx:
         keep = ctx.enter_context(tc.tile_pool(name="keep", bufs=1))
         stage = ctx.enter_context(tc.tile_pool(name="stage", bufs=1))
+        over = ctx.enter_context(tc.tile_pool(name="over", bufs=1))
         work = ctx.enter_context(tc.tile_pool(name="work", bufs=2))
         psum = ctx.enter_context(tc.psum_pool(name="psum", bufs=4))
 
@@ -41,7 +42,10 @@ def tile_list_electrolyser_sweep_pairs_kernel(
             return keep.tile(shape, dtype, name=name, align_bytes=64)
 
         def load_rows(src, slot):
-            raw = stage.tile([P, PACK, HALF], F32, name="raw", tag=slot)
+            if slot is None:
+                raw = over.tile([P, PACK, HALF], F32, name="over_raw", offset=0)
+            else:
+                raw = stage.tile([P, PACK, HALF], F32, name="raw", tag=slot, align_bytes=64)
             nc.sync.dma_start(out=raw[:], in_=src.rearrange("(p j) c -> p j c", j=PACK))
             return raw
 
@@ -54,11 +58,17 @@ def tile_list_electrolyser_sweep_pairs_kernel(
             )
             return wb
 
-        def quantise(src, name):
+        def quantise(src, name, parts=1):
             width = src.shape[1] // PACK
             codes = kept([P, width], U32, name + "_codes")
             scales = kept([P, width], U8, name + "_scales")
-            nc.vector.quantize_mx(out=codes[:].bitcast(FP8X4), scales=scales[:], in_=src)
+            step = width // parts
+            for c in range(0, width, step):
+                nc.vector.quantize_mx(
+                    out=codes[:, c : c + step].bitcast(FP8X4),
+                    scales=scales[:, c : c + step],
+                    in_=src[:, PACK * c : PACK * (c + step)],
+                )
             return codes, scales
 
         def woven(ap):
@@ -70,7 +80,7 @@ def tile_list_electrolyser_sweep_pairs_kernel(
         def cols(t):
             return slice(t * P, (t + 1) * P)
 
-        tab_s = stage.tile([P, T], U8, name="tab_s", tag="c")
+        tab_s = kept([P, T], U8, "tab_s")
         nc.vector.memset(tab_s[:].bitcast(I32), 0)
         ws_raw = kept([P, 2, PASS], U8, "ws_raw")
         nc.gpsimd.memset(ws_raw[:].bitcast(I32), 0)
@@ -89,8 +99,6 @@ def tile_list_electrolyser_sweep_pairs_kernel(
                 out=tab_s[32 * q : 32 * q + 4, :].bitcast(I32),
                 in_=tab_scales[0, 4 * q : 4 * q + 4, :].bitcast(I32),
             )
-        tab_w = stage.tile([P, T], I32, name="tab_w", tag="d")
-        nc.sync.dma_start(out=tab_w[:], in_=tab_words[0].rearrange("p t i -> p (t i)").bitcast(I32))
 
         for q in range(QUADS):
             nc.gpsimd.dma_start(
@@ -102,15 +110,18 @@ def tile_list_electrolyser_sweep_pairs_kernel(
                 in_=w3_scales[0, 4 * q : 4 * q + 4, :].bitcast(I32),
             )
 
-        twice = stage.tile([P, 2, PACK], F32, name="twice", tag="b")
+        twice = over.tile([P, 2, PACK], F32, name="twice", offset=0)
         nc.vector.tensor_scalar(twice[:], gain_t[:], 0.0, 2.0, ALU.is_ge, ALU.mult)
         sign = kept([P, 2, SIGN_COLS, PACK], BF16, "sign")
         nc.vector.tensor_scalar(
             sign[:], twice[:].unsqueeze(2).to_broadcast([P, 2, SIGN_COLS, PACK]), -1.0, None, ALU.add
         )
 
-        raw_2a = load_rows(w2[:, 0:PASS], "b")
-        w1q = {0: quantise(round_weight(raw_1a, nc.scalar.copy)[:], "w1a")}
+        tab_w = over.tile([P, T], I32, name="tab_w", offset=0)
+        nc.sync.dma_start(out=tab_w[:], in_=tab_words[0].rearrange("p t i -> p (t i)").bitcast(I32))
+        wb_1a = stage.tile([P, PACK * PASS], BF16, name="wb_1a", tag="b", align_bytes=64)
+        w1q = {0: quantise(round_weight(raw_1a, nc.scalar.copy, wb_1a)[:], "w1a")}
+        raw_2a = load_rows(w2[:, 0:PASS], "a")
         v_s = [kept([P, HALF], U8, "v_s%d" % s) for s in range(2)]
         v_w = [kept([P, HALF], U32, "v_w%d" % s) for s in range(2)]
 
@@ -136,28 +147,40 @@ def tile_list_electrolyser_sweep_pairs_kernel(
                 stop=True,
             )
 
-        def magnitudes(b, s, c0, width, order):
-            sq = [work.tile([P, PACK, width], F32, name="sq%d" % part) for part in range(2)]
-            for part, t in order:
-                bank = psum.tile([P, width], F32, name="reim")
-                stage1(bank[:], (w1q, w2q)[part][b], t, s, c0, width)
-                nc.scalar.activation(sq[part][:, t, :], bank[:], ACT.Square, scale=gain_t[:, b, t : t + 1])
-                if part == 1:
-                    nc.vector.tensor_tensor(sq[0][:, t, :], sq[0][:, t, :], sq[1][:, t, :], ALU.add)
-            hb = work.tile([P, PACK * width], BF16, name="hb", align_bytes=64)
-            nc.scalar.activation(woven(hb[:]), planes(sq[0][:]), ACT.Sqrt)
-            run = SIGN_COLS * PACK
-            reps = PACK * width // run
-            hv = hb[:].rearrange("p (r x) -> p r x", x=run)
-            nc.vector.tensor_tensor(
-                hv, hv,
-                sign[:, b].rearrange("p c t -> p (c t)").unsqueeze(1).to_broadcast([P, reps, run]),
-                ALU.mult,
-            )
-            return quantise(hb[:], "h%d%d_%d" % (b, s, c0))
+        def squares(sq, b, s, c0, order):
+            width = sq.shape[3]
+            for parts, t in order:
+                bank = psum.tile([P, len(parts), width], F32, name="reim")
+                for place, part in enumerate(parts):
+                    stage1(bank[:, place, :], (w1q, w2q)[part][b], t, s, c0, width)
+                nc.scalar.activation(
+                    sq[:, t, parts[0] : parts[-1] + 1, :], bank[:], ACT.Square, scale=gain_t[:, b, t : t + 1]
+                )
+                if parts[-1] == 1 and t % 2 == 1:
+                    both = sq[:, t - 1 : t + 1]
+                    nc.vector.tensor_tensor(both[:, :, 0, :], both[:, :, 0, :], both[:, :, 1, :], ALU.add)
 
-        re_first = [(part, t) for part in range(2) for t in range(PACK)]
-        in_turn = [(part, t) for t in range(PACK) for part in range(2)]
+        def magnitudes(sq, b, name):
+            width = sq.shape[3]
+            hb = work.tile([P, PACK * width], BF16, name="hb", align_bytes=64)
+            nc.scalar.activation(woven(hb[:]), planes(sq[:, :, 0, :]), ACT.Sqrt)
+            run = SIGN_COLS * PACK
+            span = PACK * width // 2
+            for x0 in range(0, PACK * width, span):
+                hv = hb[:, x0 : x0 + span].rearrange("p (r x) -> p r x", x=run)
+                nc.vector.tensor_tensor(
+                    hv, hv,
+                    sign[:, b].rearrange("p c t -> p (c t)").unsqueeze(1).to_broadcast([P, span // run, run]),
+                    ALU.mult,
+                )
+            return quantise(hb[:], name, 2)
+
+        def sq_tile(width):
+            return work.tile([P, PACK, 2, width], F32, name="sq")
+
+        re_first = [((part,), t) for part in range(2) for t in range(PACK)]
+        in_turn = [((part,), t) for t in range(PACK) for part in range(2)]
+        together = [((0, 1), t) for t in range(PACK)]
 
         def weighted(s, load_raw, w3q):
             bb = work.tile([P, PACK * HALF], BF16, name="bb", align_bytes=64)
@@ -171,48 +194,7 @@ def tile_list_electrolyser_sweep_pairs_kernel(
                     planes(load_raw[:, :, cols(c)]),
                     ALU.mult,
                 )
-            return quantise(bb[:], "b%d" % s)
-
-        hq = {}
-        hq[0, 0] = magnitudes(0, 0, 0, HALF, re_first)
-
-        raw_1b = load_rows(w1[:, PASS:H], "a")
-        raw_2b = load_rows(w2[:, PASS:H], "c")
-        w3_raw = stage.tile([P, M], I32, name="w3_raw", tag="b")
-        nc.sync.dma_start(out=w3_raw[:], in_=w3_words[0].rearrange("p c i -> p (c i)").bitcast(I32))
-        load_0 = load_rows(load[:, 0:HALF], "d")
-        w1q[1] = quantise(round_weight(raw_1b, nc.vector.tensor_copy)[:], "w1b")
-        w2q[1] = quantise(round_weight(raw_2b, nc.vector.tensor_copy)[:], "w2b")
-        raw_5 = load_rows(w5, "a")
-        load_1 = load_rows(load[:, HALF:S], "c")
-
-        ws = stage.tile([P, 2, PASS], U8, name="ws", tag="e", align_bytes=64)
-        nc.vector.tensor_copy(
-            out=ws[:].rearrange("p a (t q) -> p a q t", t=PACK),
-            in_=ws_raw[:].rearrange("p a (q t) -> p a q t", t=PACK),
-        )
-        w3_w = kept([P, M], I32, "w3_w")
-        nc.vector.tensor_copy(
-            out=w3_w[:].rearrange("p (t q) -> p q t", t=PACK),
-            in_=w3_raw[:].rearrange("p (q t) -> p q t", t=PACK),
-        )
-        w3q = (w3_w, ws[4:P, 0, :])
-        w4_raw = stage.tile([P, 2, N // 2], I32, name="w4_raw", tag="b")
-        nc.sync.dma_start(out=w4_raw[:], in_=w4_words.rearrange("a p c -> p a c").bitcast(I32))
-
-        hq[0, 1] = magnitudes(0, 1, 0, HALF, in_turn)
-        bq = {0: weighted(0, load_0, w3q)}
-
-        hq[1, 0] = magnitudes(1, 0, 0, HALF, in_turn)
-        w5q = quantise(round_weight(raw_5, nc.vector.tensor_copy)[:], "w5")
-        w4_w = kept([P, 2, 2 * N], U8, "w4_w")
-        nc.vector.tensor_copy(
-            out=w4_w[:].bitcast(U16).rearrange("p a (t q) -> p a q t", t=PACK),
-            in_=w4_raw[:].bitcast(U16).rearrange("p a (q t) -> p a q t", t=PACK),
-        )
-        bq[1] = weighted(1, load_1, w3q)
-
-        g2 = [kept([P, S], F32, "g2_%d" % t) for t in range(PACK)]
+            return quantise(bb[:], "b%d" % s, 2)
 
         def with_b(bank, t, s):
             nc.tensor.matmul_mx(
@@ -236,25 +218,81 @@ def tile_list_electrolyser_sweep_pairs_kernel(
                 stop=last,
             )
 
-        for t in range(PACK):
-            bank = psum.tile([P, HALF], F32, name="acc")
-            with_b(bank, t, 0)
-            with_h(bank[:], t, 0, hq[0, 0], False)
-            with_h(bank[:], t, 1, hq[1, 0], True)
-            nc.scalar.copy(g2[t][:, 0:HALF], bank[:])
+        hq = {}
+        bq = {}
+        g2 = [kept([P, S], F32, "g2_%d" % t) for t in range(PACK)]
+
+        sq_00 = sq_tile(HALF)
+        squares(sq_00, 0, 0, 0, re_first)
+
+        raw_1b = load_rows(w1[:, PASS:H], "b")
+        w3_raw = over.tile([P, M], I32, name="w3_raw", offset=8192)
+        nc.sync.dma_start(out=w3_raw[:], in_=w3_words[0].rearrange("p c i -> p (c i)").bitcast(I32))
+        load_0 = load_rows(load[:, 0:HALF], None)
+        raw_2b = load_rows(w2[:, PASS:H], "a")
+        w4_raw = over.tile([P, 2, N // 2], I32, name="w4_raw", offset=10240)
+        nc.sync.dma_start(out=w4_raw[:], in_=w4_words.rearrange("a p c -> p a c").bitcast(I32))
+
+        sq_01 = sq_tile(HALF)
+        squares(sq_01, 0, 1, 0, in_turn[:PACK])
+        hq[0, 0] = magnitudes(sq_00, 0, "h00")
+        w1q[1] = quantise(round_weight(raw_1b, nc.vector.tensor_copy)[:], "w1b")
+        raw_5 = load_rows(w5, "b")
+        squares(sq_01, 0, 1, 0, in_turn[PACK:])
+        w2q[1] = quantise(round_weight(raw_2b, nc.vector.tensor_copy)[:], "w2b")
+        load_1 = load_rows(load[:, HALF:S], "a")
+
+        ws = stage.tile([P, 2, PASS], U8, name="ws", tag="e", align_bytes=64)
+        nc.vector.tensor_copy(
+            out=ws[:].rearrange("p a (t q) -> p a q t", t=PACK),
+            in_=ws_raw[:].rearrange("p a (q t) -> p a q t", t=PACK),
+        )
+        w3_w = kept([P, M], I32, "w3_w")
+        nc.vector.tensor_copy(
+            out=w3_w[:].rearrange("p (t q) -> p q t", t=PACK),
+            in_=w3_raw[:].rearrange("p (q t) -> p q t", t=PACK),
+        )
+        w3q = (w3_w, ws[4:P, 0, :])
+
+        sq_10 = sq_tile(HALF)
+        squares(sq_10, 1, 0, 0, in_turn[:PACK])
+        hq[0, 1] = magnitudes(sq_01, 0, "h01")
+        bq[0] = weighted(0, load_0, w3q)
+        squares(sq_10, 1, 0, 0, in_turn[PACK:])
+        w5q = quantise(round_weight(raw_5, nc.vector.tensor_copy)[:], "w5")
+        w4_w = kept([P, 2, 2 * N], U8, "w4_w")
+        nc.vector.tensor_copy(
+            out=w4_w[:].bitcast(U16).rearrange("p a (t q) -> p a q t", t=PACK),
+            in_=w4_raw[:].bitcast(U16).rearrange("p a (q t) -> p a q t", t=PACK),
+        )
 
         quarter = HALF // 2
-        h_last = [magnitudes(1, 1, 0, quarter, in_turn)]
-        banks = []
+        sq_a = sq_tile(quarter)
+        squares(sq_a, 1, 1, 0, together[:2])
+        hq[1, 0] = magnitudes(sq_10, 1, "h10")
+        squares(sq_a, 1, 1, 0, together[2:])
+        bq[1] = weighted(1, load_1, w3q)
+        sq_b = sq_tile(quarter)
+        squares(sq_b, 1, 1, quarter, together)
+        early = []
         for t in range(PACK):
-            banks.append(psum.tile([P, HALF], F32, name="acc"))
-            with_b(banks[t], t, 1)
-            with_h(banks[t][:], t, 0, hq[0, 1], False)
-            with_h(banks[t][:, 0:quarter], t, 1, h_last[0], False)
-        h_last.append(magnitudes(1, 1, quarter, quarter, in_turn))
+            early.append(psum.tile([P, HALF], F32, name="acc"))
+            with_b(early[t], t, 0)
+            with_h(early[t][:], t, 0, hq[0, 0], False)
+            with_h(early[t][:], t, 1, hq[1, 0], True)
+        h_a = magnitudes(sq_a, 1, "h11a")
+        for t in range(2):
+            nc.scalar.copy(g2[t][:, 0:HALF], early[t][:])
+        h_b = magnitudes(sq_b, 1, "h11b")
+        for t in range(2, PACK):
+            nc.scalar.copy(g2[t][:, 0:HALF], early[t][:])
         for t in range(PACK):
-            with_h(banks[t][:, quarter:HALF], t, 1, h_last[1], True)
-            nc.scalar.copy(g2[t][:, HALF:S], banks[t][:])
+            late = psum.tile([P, HALF], F32, name="acc")
+            with_b(late, t, 1)
+            with_h(late[:], t, 0, hq[0, 1], False)
+            with_h(late[:, 0:quarter], t, 1, h_a, False)
+            with_h(late[:, quarter:HALF], t, 1, h_b, True)
+            nc.scalar.copy(g2[t][:, HALF:S], late[:])
 
         y_codes = kept([P, PAIRS], U32, "y_codes")
         y_scales = kept([P, PAIRS], U8, "y_scales")

from contextlib import ExitStack

import concourse.mybir as mybir

K, T, S, H, M, N, PAIRS = 512, 4096, 1024, 1024, 512, 512, 512
FLOPS = 2 * K * S * (2 * H + M) + 2 * S * N * (H + M)

F32 = mybir.dt.float32
BF16 = mybir.dt.bfloat16
I32 = mybir.dt.int32
U32 = mybir.dt.uint32
U16 = mybir.dt.uint16
U8 = mybir.dt.uint8
FP8X4 = mybir.dt.float8_e4m3fn_x4
FP4X4 = mybir.dt.float4_e2m1fn_x4
ALU = mybir.AluOpType
ACT = mybir.ActivationFunctionType

P = 128
PACK = 4
PASS = P * PACK
HALF = 512
LIST_ROWS = 16
QUADS = 4
SIGN_COLS = 64
PAIR_PIECES = (256, 128, 128)


def tile_list_electrolyser_sweep_pairs_kernel(
    tc, tab_words, tab_scales, offs, pos1, pos2, w1, w2, gain, w3_words, w3_scales, load,
    w4_words, w4_scales, w5, out_0, out_1, out_2,
):
    nc = tc.nc
    with ExitStack() as ctx:
        keep = ctx.enter_context(tc.tile_pool(name="keep", bufs=1))
        stage = ctx.enter_context(tc.tile_pool(name="stage", bufs=1))
        over = ctx.enter_context(tc.tile_pool(name="over", bufs=1))
        work = ctx.enter_context(tc.tile_pool(name="work", bufs=2))
        psum = ctx.enter_context(tc.psum_pool(name="psum", bufs=4))

        def kept(shape, dtype, name):
            return keep.tile(shape, dtype, name=name, align_bytes=64)

        def load_rows(src, slot):
            if slot is None:
                raw = over.tile([P, PACK, HALF], F32, name="over_raw", offset=0)
            else:
                raw = stage.tile([P, PACK, HALF], F32, name="raw", tag=slot, align_bytes=64)
            nc.sync.dma_start(out=raw[:], in_=src.rearrange("(p j) c -> p j c", j=PACK))
            return raw

        def round_weight(raw, copy, wb=None):
            if wb is None:
                wb = work.tile([P, PACK * PASS], BF16, name="wb", align_bytes=64)
            copy(
                out=wb[:].rearrange("p (t m j) -> p m j t", t=PACK, j=PACK),
                in_=raw[:].rearrange("p j (m t) -> p m j t", t=PACK),
            )
            return wb

        def quantise(src, name, parts=1):
            width = src.shape[1] // PACK
            codes = kept([P, width], U32, name + "_codes")
            scales = kept([P, width], U8, name + "_scales")
            step = width // parts
            for c in range(0, width, step):
                nc.vector.quantize_mx(
                    out=codes[:, c : c + step].bitcast(FP8X4),
                    scales=scales[:, c : c + step],
                    in_=src[:, PACK * c : PACK * (c + step)],
                )
            return codes, scales

        def woven(ap):
            return ap.rearrange("p (c i t) -> p c t i", t=PACK, i=PACK)

        def planes(ap):
            return ap.rearrange("p t (c i) -> p c t i", i=PACK)

        def cols(t):
            return slice(t * P, (t + 1) * P)

        tab_s = kept([P, T], U8, "tab_s")
        nc.vector.memset(tab_s[:].bitcast(I32), 0)
        ws_raw = kept([P, 2, PASS], U8, "ws_raw")
        nc.gpsimd.memset(ws_raw[:].bitcast(I32), 0)

        offs_t = keep.tile([P, S // LIST_ROWS], U16, name="offs_t")
        nc.sync.dma_start(offs_t[:], offs)
        gain_t = kept([P, 2, PACK], F32, "gain_t")
        nc.sync.dma_start(out=gain_t[:], in_=gain.rearrange("(b p t) -> p b t", b=2, t=PACK))
        pos_t = []
        for name, src in (("pos1_t", pos1), ("pos2_t", pos2)):
            pos_t.append(keep.tile([P, PAIRS // LIST_ROWS], U16, name=name))
            nc.sync.dma_start(pos_t[-1][:], src)
        raw_1a = load_rows(w1[:, 0:PASS], "a")
        for q in range(QUADS):
            nc.scalar.dma_start(
                out=tab_s[32 * q : 32 * q + 4, :].bitcast(I32),
                in_=tab_scales[0, 4 * q : 4 * q + 4, :].bitcast(I32),
            )

        for q in range(QUADS):
            nc.gpsimd.dma_start(
                out=ws_raw[32 * q : 32 * q + 4, :, :].bitcast(I32),
                in_=w4_scales[:, 4 * q : 4 * q + 4, :].rearrange("a r c -> r a c").bitcast(I32),
            )
            nc.gpsimd.dma_start(
                out=ws_raw[32 * q + 4 : 32 * q + 8, 0, :].bitcast(I32),
                in_=w3_scales[0, 4 * q : 4 * q + 4, :].bitcast(I32),
            )

        twice = over.tile([P, 2, PACK], F32, name="twice", offset=0)
        nc.vector.tensor_scalar(twice[:], gain_t[:], 0.0, 2.0, ALU.is_ge, ALU.mult)
        sign = kept([P, 2, SIGN_COLS, PACK], BF16, "sign")
        nc.vector.tensor_scalar(
            sign[:], twice[:].unsqueeze(2).to_broadcast([P, 2, SIGN_COLS, PACK]), -1.0, None, ALU.add
        )

        tab_w = over.tile([P, T], I32, name="tab_w", offset=0)
        nc.sync.dma_start(out=tab_w[:], in_=tab_words[0].rearrange("p t i -> p (t i)").bitcast(I32))
        wb_1a = stage.tile([P, PACK * PASS], BF16, name="wb_1a", tag="b", align_bytes=64)
        w1q = {0: quantise(round_weight(raw_1a, nc.scalar.copy, wb_1a)[:], "w1a")}
        raw_2a = load_rows(w2[:, 0:PASS], "a")
        v_s = [kept([P, HALF], U8, "v_s%d" % s) for s in range(2)]
        v_w = [kept([P, HALF], U32, "v_w%d" % s) for s in range(2)]

        def gather_words(s):
            per = HALF // LIST_ROWS
            entries = offs_t[:, s * per : (s + 1) * per]
            nc.vector.tensor_copy(v_s[s][:], tab_s[:].indirect(entries))
            nc.vector.tensor_copy(v_w[s][:], tab_w[:].bitcast(U32).indirect(entries))

        gather_words(0)
        wb_2a = stage.tile([P, PACK * PASS], BF16, name="wb_2a", tag="e", align_bytes=64)
        w2q = {0: quantise(round_weight(raw_2a, nc.vector.tensor_copy, wb_2a)[:], "w2a")}
        gather_words(1)

        def stage1(out, wq, t, s, c0, width):
            nc.tensor.matmul_mx(
                out=out,
                lhsT=wq[0][:, cols(t)].bitcast(FP8X4),
                lhsT_scale=wq[1][:, cols(t)],
                rhs=v_w[s][:, c0 : c0 + width].bitcast(FP8X4),
                rhs_scale=v_s[s][:, c0 : c0 + width],
                start=True,
                stop=True,
            )

        def squares(sq, b, s, c0, order):
            width = sq.shape[3]
            for parts, t in order:
                bank = psum.tile([P, len(parts), width], F32, name="reim")
                for place, part in enumerate(parts):
                    stage1(bank[:, place, :], (w1q, w2q)[part][b], t, s, c0, width)
                nc.scalar.activation(
                    sq[:, t, parts[0] : parts[-1] + 1, :], bank[:], ACT.Square, scale=gain_t[:, b, t : t + 1]
                )
                if parts[-1] == 1 and t % 2 == 1:
                    both = sq[:, t - 1 : t + 1]
                    nc.vector.tensor_tensor(both[:, :, 0, :], both[:, :, 0, :], both[:, :, 1, :], ALU.add)

        def magnitudes(sq, b, name):
            width = sq.shape[3]
            hb = work.tile([P, PACK * width], BF16, name="hb", align_bytes=64)
            nc.scalar.activation(woven(hb[:]), planes(sq[:, :, 0, :]), ACT.Sqrt)
            run = SIGN_COLS * PACK
            span = PACK * width // 2
            for x0 in range(0, PACK * width, span):
                hv = hb[:, x0 : x0 + span].rearrange("p (r x) -> p r x", x=run)
                nc.vector.tensor_tensor(
                    hv, hv,
                    sign[:, b].rearrange("p c t -> p (c t)").unsqueeze(1).to_broadcast([P, span // run, run]),
                    ALU.mult,
                )
            return quantise(hb[:], name, 2)

        def sq_tile(width):
            return work.tile([P, PACK, 2, width], F32, name="sq")

        re_first = [((part,), t) for part in range(2) for t in range(PACK)]
        in_turn = [((part,), t) for t in range(PACK) for part in range(2)]
        together = [((0, 1), t) for t in range(PACK)]

        def weighted(s, load_raw, w3q):
            bb = work.tile([P, PACK * HALF], BF16, name="bb", align_bytes=64)
            for c in range(HALF // P):
                bank = psum.tile([P, PACK, P], F32, name="acc")
                for t in range(PACK):
                    stage1(bank[:, t, :], w3q, t, s, c * P, P)
                nc.vector.tensor_tensor(
                    woven(bb[:, c * PASS : (c + 1) * PASS]),
                    planes(bank[:]),
                    planes(load_raw[:, :, cols(c)]),
                    ALU.mult,
                )
            return quantise(bb[:], "b%d" % s, 2)

        def with_b(bank, t, s):
            nc.tensor.matmul_mx(
                out=bank[:],
                lhsT=w5q[0][:, cols(t)].bitcast(FP8X4),
                lhsT_scale=w5q[1][:, cols(t)],
                rhs=bq[s][0][:].bitcast(FP8X4),
                rhs_scale=bq[s][1][:],
                start=True,
                stop=False,
            )

        def with_h(out, t, b, h, last):
            nc.tensor.matmul_mx(
                out=out,
                lhsT=w4_w[:, b, 2 * t * P : 2 * (t + 1) * P].bitcast(FP4X4),
                lhsT_scale=ws[:, b, cols(t)],
                rhs=h[0][:].bitcast(FP8X4),
                rhs_scale=h[1][:],
                start=False,
                stop=last,
            )

        hq = {}
        bq = {}
        g2 = [kept([P, S], F32, "g2_%d" % t) for t in range(PACK)]

        sq_00 = sq_tile(HALF)
        squares(sq_00, 0, 0, 0, re_first)

        raw_1b = load_rows(w1[:, PASS:H], "b")
        w3_raw = over.tile([P, M], I32, name="w3_raw", offset=8192)
        nc.sync.dma_start(out=w3_raw[:], in_=w3_words[0].rearrange("p c i -> p (c i)").bitcast(I32))
        load_0 = load_rows(load[:, 0:HALF], None)
        raw_2b = load_rows(w2[:, PASS:H], "a")
        w4_raw = over.tile([P, 2, N // 2], I32, name="w4_raw", offset=10240)
        nc.sync.dma_start(out=w4_raw[:], in_=w4_words.rearrange("a p c -> p a c").bitcast(I32))

        sq_01 = sq_tile(HALF)
        squares(sq_01, 0, 1, 0, in_turn[:PACK])
        hq[0, 0] = magnitudes(sq_00, 0, "h00")
        w1q[1] = quantise(round_weight(raw_1b, nc.vector.tensor_copy)[:], "w1b")
        raw_5 = load_rows(w5, "b")
        squares(sq_01, 0, 1, 0, in_turn[PACK:])
        w2q[1] = quantise(round_weight(raw_2b, nc.vector.tensor_copy)[:], "w2b")
        load_1 = load_rows(load[:, HALF:S], "a")

        ws = stage.tile([P, 2, PASS], U8, name="ws", tag="e", align_bytes=64)
        nc.vector.tensor_copy(
            out=ws[:].rearrange("p a (t q) -> p a q t", t=PACK),
            in_=ws_raw[:].rearrange("p a (q t) -> p a q t", t=PACK),
        )
        w3_w = kept([P, M], I32, "w3_w")
        nc.vector.tensor_copy(
            out=w3_w[:].rearrange("p (t q) -> p q t", t=PACK),
            in_=w3_raw[:].rearrange("p (q t) -> p q t", t=PACK),
        )
        w3q = (w3_w, ws[4:P, 0, :])

        sq_10 = sq_tile(HALF)
        squares(sq_10, 1, 0, 0, in_turn[:PACK])
        hq[0, 1] = magnitudes(sq_01, 0, "h01")
        bq[0] = weighted(0, load_0, w3q)
        squares(sq_10, 1, 0, 0, in_turn[PACK:])
        w5q = quantise(round_weight(raw_5, nc.vector.tensor_copy)[:], "w5")
        w4_w = kept([P, 2, 2 * N], U8, "w4_w")
        nc.vector.tensor_copy(
            out=w4_w[:].bitcast(U16).rearrange("p a (t q) -> p a q t", t=PACK),
            in_=w4_raw[:].bitcast(U16).rearrange("p a (q t) -> p a q t", t=PACK),
        )

        quarter = HALF // 2
        sq_a = sq_tile(quarter)
        squares(sq_a, 1, 1, 0, together[:2])
        hq[1, 0] = magnitudes(sq_10, 1, "h10")
        squares(sq_a, 1, 1, 0, together[2:])
        bq[1] = weighted(1, load_1, w3q)
        sq_b = sq_tile(quarter)
        squares(sq_b, 1, 1, quarter, together)
        early = []
        for t in range(PACK):
            early.append(psum.tile([P, HALF], F32, name="acc"))
            with_b(early[t], t, 0)
            with_h(early[t][:], t, 0, hq[0, 0], False)
            with_h(early[t][:], t, 1, hq[1, 0], True)
        h_a = magnitudes(sq_a, 1, "h11a")
        for t in range(2):
            nc.scalar.copy(g2[t][:, 0:HALF], early[t][:])
        h_b = magnitudes(sq_b, 1, "h11b")
        for t in range(2, PACK):
            nc.scalar.copy(g2[t][:, 0:HALF], early[t][:])
        for t in range(PACK):
            late = psum.tile([P, HALF], F32, name="acc")
            with_b(late, t, 1)
            with_h(late[:], t, 0, hq[0, 1], False)
            with_h(late[:, 0:quarter], t, 1, h_a, False)
            with_h(late[:, quarter:HALF], t, 1, h_b, True)
            nc.scalar.copy(g2[t][:, HALF:S], late[:])

        y_codes = kept([P, PAIRS], U32, "y_codes")
        y_scales = kept([P, PAIRS], U8, "y_scales")
        out_rows = out_0.rearrange("(p t) j -> p t j", t=PACK)
        out_words = out_1[0].rearrange("p m t -> p (m t)").bitcast(I32)
        j0 = 0
        for piece, width in enumerate(PAIR_PIECES):
            entries = slice(j0 // LIST_ROWS, (j0 + width) // LIST_ROWS)
            first = kept([P, PACK, width], F32, "first%d" % piece)
            y = kept([P, PACK, width], F32, "y%d" % piece)
            for t in range(PACK):
                nc.vector.tensor_copy(first[:, t, :], g2[t][:].indirect(pos_t[0][:, entries]))
            for t in range(PACK):
                nc.vector.tensor_tensor(
                    y[:, t, :], g2[t][:].indirect(pos_t[1][:, entries]), first[:, t, :], ALU.mult
                )
            nc.sync.dma_start(out=out_rows[:, :, j0 : j0 + width], in_=y[:])
            yb = kept([P, PACK * width], BF16, "yb%d" % piece)
            nc.scalar.copy(woven(yb[:]), planes(y[:]))
            nc.vector.quantize_mx(
                out=y_codes[:, j0 : j0 + width].bitcast(FP8X4),
                scales=y_scales[:, j0 : j0 + width],
                in_=yb[:],
            )
            nc.sync.dma_start(
                out=out_words[:, j0 : j0 + width], in_=y_codes[:, j0 : j0 + width].bitcast(I32)
            )
            j0 = j0 + width
        for q in range(QUADS):
            (nc.sync, nc.scalar)[q % 2].dma_start(
                out=out_2[0, 4 * q : 4 * q + 4, :].bitcast(I32),
                in_=y_scales[32 * q : 32 * q + 4, :].bitcast(I32),
            )
